import numpy as np, ml_dtypes
CORES = [61,69,101,62,70,102]
N = 6
KB, QP, ROOT = 2, 32, 2
def setup_inputs(rng):
    return {"q": rng.standard_normal((N, 128, QP), dtype=np.float32).astype(ml_dtypes.bfloat16), "k": rng.standard_normal((N, 128, KB * 128), dtype=np.float32).astype(ml_dtypes.bfloat16), "v": rng.standard_normal((N, 128, KB * 128), dtype=np.float32).astype(ml_dtypes.bfloat16)}
def setup_inputs_big(rng):
    d = setup_inputs(rng)
    for k in ("q", "k", "v"): d[k] = (d[k].astype(np.float32) * 1024.0).astype(d[k].dtype)
    return d
def setup_inputs_small(rng):
    d = setup_inputs(rng)
    for k in ("q", "k", "v"): d[k] = (d[k].astype(np.float32) * (1 / 1024.0)).astype(d[k].dtype)
    return d
def setup_inputs_apart(rng):
    d = setup_inputs(rng)
    f = (10.0 ** rng.permutation(np.linspace(-1.5, 1.5, N))).astype(np.float32).reshape(N, 1, 1)
    for k in ("q", "k", "v"): d[k] = (d[k].astype(np.float32) * f).astype(d[k].dtype)
    return d
def reference(q, k, v):
    Q, K, V = q.astype(np.float64), k.astype(np.float64), v.astype(np.float64)
    o = np.zeros((128, QP))
    for j in range(N):
        for b in range(KB):
            o += V[j][:, 128 * b:128 * b + 128].T @ np.maximum(K[j][:, 128 * b:128 * b + 128].T @ Q[ROOT], 0.0)
    y = np.full((N, 128, QP), np.nan)
    y[ROOT] = o
    return {"y": y.astype(ml_dtypes.bfloat16 if q.dtype != np.float64 else np.float64)}

@@ -1,0 +1,154 @@
+from concourse.bass import DstId, RemoteDMATransfer
+from concourse.mybir import AluOpType
+
+P = 128
+KB = 2
+QP = 32
+W = KB * P
+SLOT = 2 * W
+NSLOT = 2
+NLAND = 3
+
+SCRATCH = {
+    "qs": ("sbuf", [P, QP], "bfloat16"),
+    "kv": ("sbuf", [P, NSLOT * SLOT], "bfloat16"),
+    "zero": ("sbuf", [P, NSLOT * KB * QP], "bfloat16"),
+    "ssb": ("sbuf", [P, NSLOT * KB * QP], "bfloat16"),
+    "osb": ("sbuf", [P, QP], "bfloat16"),
+    "oland": ("sbuf", [P, NLAND * QP], "bfloat16"),
+    "acc": ("sbuf", [P, NLAND * QP], "float32"),
+    "sps": ("psum", [P, 512], "float32"),
+    "ops": ("psum", [P, 512], "float32"),
+}
+SEMAPHORES = ["qin", "kld", "vld", "guest", "sent", "zset", "mm1", "relu", "mm2", "odone", "vadd",
+              "land0", "land1", "land2", "stored"]
+
+
+def _count(mask):
+    return bin(mask).count("1")
+
+
+def _plan(T, topo):
+    cores = list(T.cores)
+    root = cores[T.root]
+    others = [c for c in cores if c != root]
+    near = [c for c in others if topo.chip(c) == topo.chip(root)]
+    away = [c for c in others if topo.chip(c) != topo.chip(root)]
+    direct = [c for c in away if topo.may_write(root, c) and topo.may_write(c, root)]
+    far = [c for c in away if c not in direct]
+    collector = [c for c in far if topo.may_write(c, root)][0]
+    feeders = [c for c in far if c != collector]
+    porter = [c for c in near if topo.may_write(c, collector)][0]
+    return root, porter, direct, collector, feeders
+
+
+def _send(g, T, topo, src, dst, out_ap, in_ap, remote_sem, mask):
+    rid, pid, _ = topo.addr(dst)
+    g.remote_dma(out_ap, in_ap, remote_sem, T.sem.sent, pid, rid, mask)
+    return _count(mask)
+
+
+def _load_kv(g, T):
+    g.sync.dma_start(T.kv[:, 0:W], T.k[:]).then_inc(T.sem.kld, 16)
+    g.scalar.dma_start(T.kv[:, W:SLOT], T.v[:]).then_inc(T.sem.vld, 16)
+
+
+def _attend(g, T, nslots, waits):
+    te, ve = g.tensor, g.vector
+    nb = nslots * KB
+    ve.memset(T.zero[:, 0:nb * QP], 0.0).then_inc(T.sem.zset, 1)
+    for sem, val in waits:
+        te.wait_ge(sem, val)
+    for j in range(nb):
+        s, b = divmod(j, KB)
+        c = s * SLOT + b * P
+        te.matmul(T.sps[:, j * QP:(j + 1) * QP], T.kv[:, c:c + P], T.qs[:], start=True, stop=True).then_inc(T.sem.mm1, 1)
+    ve.wait_ge(T.sem.zset, 1)
+    ve.wait_ge(T.sem.mm1, nb)
+    ve.tensor_tensor(T.ssb[:, 0:nb * QP], T.sps[:, 0:nb * QP], T.zero[:, 0:nb * QP], AluOpType.max).then_inc(T.sem.relu, 1)
+    te.wait_ge(T.sem.relu, 1)
+    for j in range(nb):
+        s, b = divmod(j, KB)
+        c = s * SLOT + W + b * P
+        te.matmul(T.ops[:, 0:QP], T.kv[:, c:c + P], T.ssb[:, j * QP:(j + 1) * QP],
+                  start=(j == 0), stop=(j == nb - 1)).then_inc(T.sem.mm2, 1)
+    ve.wait_ge(T.sem.mm2, nb)
+    return nb
+
+
+def _return_result(g, T, topo, core, root, slot):
+    g.vector.tensor_copy(T.osb[:], T.ops[:, 0:QP]).then_inc(T.sem.odone, 1)
+    g.wait_ge(T.sem.odone, 1)
+    n = _send(g, T, topo, core, root, T.oland[:, slot * QP:(slot + 1) * QP], T.osb[:],
+              T.sem["land%d" % slot], topo.mask(core, root))
+    g.wait_ge(T.sem.sent, n)
+
+
+def rank_program(g, core, T, topo):
+    if T.rank_of(core) is None:
+        return
+    root, porter, direct, collector, feeders = _plan(T, topo)
+    senders = direct + [collector]
+
+    if core == root:
+        off = topo.mask(root, direct[0])
+        on_only = topo.mask(root, porter) & ~off
+        g.sync.dma_start(T.qs[:], T.q[:]).then_inc(T.sem.qin, 16)
+        g.wait_ge(T.sem.qin, 16)
+        n = _send(g, T, topo, root, porter, T.qs[:], T.qs[:], T.sem.qin, on_only)
+        ids = [DstId(rid=topo.addr(d)[0], pnc=topo.addr(d)[1]) for d in direct]
+        g.remote_dma_fused([RemoteDMATransfer(dst_ids=ids, dma_engine_mask=off, remote_sem=T.sem.qin,
+                                              srcs=[T.qs[:]], dsts=[T.qs[:] for _ in direct])],
+                           local_sem=T.sem.sent)
+        n += _count(off)
+        g.sync.wait_ge(T.sem.sent, n)
+        g.scalar.wait_ge(T.sem.sent, n)
+        _load_kv(g, T)
+        g.wait_ge(T.sem.sent, n)
+        guest = 2 * _count(topo.mask(porter, root) & ~topo.mask(porter, collector))
+        _attend(g, T, 2, [(T.sem.qin, 16), (T.sem.kld, 16), (T.sem.vld, 16), (T.sem.guest, guest)])
+        ve = g.vector
+        prev = T.ops[:, 0:QP]
+        for i, s in enumerate(senders):
+            last = i == len(senders) - 1
+            ve.wait_ge(T.sem["land%d" % i], _count(topo.mask(s, root)))
+            if i:
+                ve.wait_ge(T.sem.vadd, i)
+            out = T.osb[:] if last else T.acc[:, i * QP:(i + 1) * QP]
+            ve.tensor_tensor(out, prev, T.oland[:, i * QP:(i + 1) * QP], AluOpType.add).then_inc(T.sem.vadd, 1)
+            prev = out
+        g.sync.wait_ge(T.sem.vadd, len(senders))
+        g.sync.dma_start(T.y[:], T.osb[:]).then_inc(T.sem.stored, 16)
+        g.sync.wait_ge(T.sem.stored, 16)
+
+    elif core == porter:
+        off = topo.mask(porter, collector)
+        on_only = topo.mask(porter, root) & ~off
+        _load_kv(g, T)
+        g.wait_ge(T.sem.kld, 16)
+        n = _send(g, T, topo, porter, root, T.kv[:, SLOT:SLOT + W], T.kv[:, 0:W], T.sem.guest, on_only)
+        g.wait_ge(T.sem.qin, _count(topo.mask(root, porter) & ~topo.mask(root, direct[0])))
+        n += _send(g, T, topo, porter, collector, T.qs[:], T.qs[:], T.sem.qin, off)
+        g.wait_ge(T.sem.vld, 16)
+        n += _send(g, T, topo, porter, root, T.kv[:, SLOT + W:2 * SLOT], T.kv[:, W:SLOT], T.sem.guest, on_only)
+        g.wait_ge(T.sem.sent, n)
+
+    elif core in feeders:
+        _load_kv(g, T)
+        g.wait_ge(T.sem.kld, 16)
+        g.wait_ge(T.sem.vld, 16)
+        n = _send(g, T, topo, core, collector, T.kv[:, SLOT:2 * SLOT], T.kv[:, 0:SLOT], T.sem.guest,
+                  topo.mask(core, collector))
+        g.wait_ge(T.sem.sent, n)
+
+    elif core == collector:
+        _load_kv(g, T)
+        guest = sum(_count(topo.mask(f, collector)) for f in feeders)
+        _attend(g, T, 2, [(T.sem.kld, 16), (T.sem.vld, 16), (T.sem.guest, guest),
+                          (T.sem.qin, _count(topo.mask(porter, collector)))])
+        _return_result(g, T, topo, core, root, senders.index(core))
+
+    else:
+        _load_kv(g, T)
+        _attend(g, T, 1, [(T.sem.kld, 16), (T.sem.vld, 16), (T.sem.qin, _count(topo.mask(root, core)))])
+        _return_result(g, T, topo, core, root, senders.index(core))

@@ -6,149 +6,174 @@ KB = 2
 QP = 32
 W = KB * P
 SLOT = 2 * W
-NSLOT = 2
-NLAND = 3
+NLAND = 2
+MAXB = 2 * KB + NLAND
 
 SCRATCH = {
+    "qd": ("dram", [P, QP], "bfloat16"),
     "qs": ("sbuf", [P, QP], "bfloat16"),
-    "kv": ("sbuf", [P, NSLOT * SLOT], "bfloat16"),
-    "zero": ("sbuf", [P, NSLOT * KB * QP], "bfloat16"),
-    "ssb": ("sbuf", [P, NSLOT * KB * QP], "bfloat16"),
+    "kv": ("sbuf", [P, 2 * SLOT + NLAND * 2 * P], "bfloat16"),
+    "zero": ("sbuf", [P, MAXB * QP], "bfloat16"),
+    "ssb": ("sbuf", [P, MAXB * QP], "bfloat16"),
     "osb": ("sbuf", [P, QP], "bfloat16"),
     "oland": ("sbuf", [P, NLAND * QP], "bfloat16"),
     "acc": ("sbuf", [P, NLAND * QP], "float32"),
-    "sps": ("psum", [P, 512], "float32"),
+    "sps0": ("psum", [P, 512], "float32"),
+    "sps1": ("psum", [P, 512], "float32"),
     "ops": ("psum", [P, 512], "float32"),
 }
-SEMAPHORES = ["qin", "kld", "vld", "guest", "sent", "zset", "mm1", "relu", "mm2", "odone", "vadd",
-              "land0", "land1", "land2", "stored"]
+SEMAPHORES = ["qcp", "qin", "kld", "vld", "guest", "passed", "sent", "zset", "mm1", "relu", "mm2", "odone", "vadd",
+              "land0", "land1", "stored"]
+Q_ENGINES = 4
 
 
 def _count(mask):
     return bin(mask).count("1")
 
 
+def _take(mask, n):
+    bits = [i for i in range(mask.bit_length()) if (mask >> i) & 1][:n]
+    return sum(1 << i for i in bits)
+
+
 def _plan(T, topo):
     cores = list(T.cores)
     root = cores[T.root]
-    others = [c for c in cores if c != root]
-    near = [c for c in others if topo.chip(c) == topo.chip(root)]
-    away = [c for c in others if topo.chip(c) != topo.chip(root)]
-    direct = [c for c in away if topo.may_write(root, c) and topo.may_write(c, root)]
-    far = [c for c in away if c not in direct]
-    collector = [c for c in far if topo.may_write(c, root)][0]
-    feeders = [c for c in far if c != collector]
-    porter = [c for c in near if topo.may_write(c, collector)][0]
-    return root, porter, direct, collector, feeders
+    porter = [c for c in cores if c != root and topo.chip(c) == topo.chip(root)][0]
+    chips = []
+    for c in cores:
+        if topo.chip(c) != topo.chip(root) and topo.chip(c) not in chips:
+            chips.append(topo.chip(c))
+    groups = []
+    for ch in chips:
+        ranks = [c for c in cores if topo.chip(c) == ch]
+        collector = [c for c in ranks if topo.may_write(c, root)][0]
+        via = root if topo.may_write(root, collector) else porter
+        groups.append((collector, [c for c in ranks if c != collector], via))
+    groups.sort(key=lambda gr: gr[2] != root)
+    return root, porter, groups
 
 
-def _send(g, T, topo, src, dst, out_ap, in_ap, remote_sem, mask):
+def _send(g, T, topo, dst, out_ap, in_ap, remote_sem, mask):
     rid, pid, _ = topo.addr(dst)
     g.remote_dma(out_ap, in_ap, remote_sem, T.sem.sent, pid, rid, mask)
     return _count(mask)
 
 
-def _load_kv(g, T):
-    g.sync.dma_start(T.kv[:, 0:W], T.k[:]).then_inc(T.sem.kld, 16)
-    g.scalar.dma_start(T.kv[:, W:SLOT], T.v[:]).then_inc(T.sem.vld, 16)
+def _slot_blocks(s):
+    return [(s * SLOT + b * P, s * SLOT + W + b * P) for b in range(KB)]
 
 
-def _attend(g, T, nslots, waits):
+def _attend(g, T, batches):
     te, ve = g.tensor, g.vector
-    nb = nslots * KB
-    ve.memset(T.zero[:, 0:nb * QP], 0.0).then_inc(T.sem.zset, 1)
-    for sem, val in waits:
-        te.wait_ge(sem, val)
-    for j in range(nb):
-        s, b = divmod(j, KB)
-        c = s * SLOT + b * P
-        te.matmul(T.sps[:, j * QP:(j + 1) * QP], T.kv[:, c:c + P], T.qs[:], start=True, stop=True).then_inc(T.sem.mm1, 1)
+    total = sum(len(blocks) for _, blocks in batches)
+    ve.memset(T.zero[:, 0:total * QP], 0.0).then_inc(T.sem.zset, 1)
     ve.wait_ge(T.sem.zset, 1)
-    ve.wait_ge(T.sem.mm1, nb)
-    ve.tensor_tensor(T.ssb[:, 0:nb * QP], T.sps[:, 0:nb * QP], T.zero[:, 0:nb * QP], AluOpType.max).then_inc(T.sem.relu, 1)
-    te.wait_ge(T.sem.relu, 1)
-    for j in range(nb):
-        s, b = divmod(j, KB)
-        c = s * SLOT + W + b * P
-        te.matmul(T.ops[:, 0:QP], T.kv[:, c:c + P], T.ssb[:, j * QP:(j + 1) * QP],
-                  start=(j == 0), stop=(j == nb - 1)).then_inc(T.sem.mm2, 1)
-    ve.wait_ge(T.sem.mm2, nb)
-    return nb
-
-
-def _return_result(g, T, topo, core, root, slot):
-    g.vector.tensor_copy(T.osb[:], T.ops[:, 0:QP]).then_inc(T.sem.odone, 1)
-    g.wait_ge(T.sem.odone, 1)
-    n = _send(g, T, topo, core, root, T.oland[:, slot * QP:(slot + 1) * QP], T.osb[:],
-              T.sem["land%d" % slot], topo.mask(core, root))
-    g.wait_ge(T.sem.sent, n)
+    done = 0
+    for i, (waits, blocks) in enumerate(batches):
+        sps = T["sps%d" % i]
+        nb = len(blocks)
+        for sem, val in waits:
+            te.wait_ge(sem, val)
+        for j, (kc, _) in enumerate(blocks):
+            te.matmul(sps[:, j * QP:(j + 1) * QP], T.kv[:, kc:kc + P], T.qs[:], start=True, stop=True).then_inc(T.sem.mm1, 1)
+        ve.wait_ge(T.sem.mm1, done + nb)
+        ve.tensor_tensor(T.ssb[:, done * QP:(done + nb) * QP], sps[:, 0:nb * QP], T.zero[:, 0:nb * QP],
+                         AluOpType.max).then_inc(T.sem.relu, 1)
+        te.wait_ge(T.sem.relu, i + 1)
+        for j, (_, vc) in enumerate(blocks):
+            n = done + j
+            te.matmul(T.ops[:, 0:QP], T.kv[:, vc:vc + P], T.ssb[:, n * QP:(n + 1) * QP],
+                      start=(n == 0), stop=(n == total - 1)).then_inc(T.sem.mm2, 1)
+        done += nb
+    ve.wait_ge(T.sem.mm2, total)
 
 
 def rank_program(g, core, T, topo):
     if T.rank_of(core) is None:
         return
-    root, porter, direct, collector, feeders = _plan(T, topo)
-    senders = direct + [collector]
+    root, porter, groups = _plan(T, topo)
+    collectors = [gr[0] for gr in groups]
+    far = [gr[0] for gr in groups if gr[2] == porter]
+    q_on = _take(topo.mask(root, collectors[0]), Q_ENGINES)
+    porter_on = topo.mask(porter, root) & ~topo.mask(porter, far[0])
 
     if core == root:
-        off = topo.mask(root, direct[0])
-        on_only = topo.mask(root, porter) & ~off
-        g.sync.dma_start(T.qs[:], T.q[:]).then_inc(T.sem.qin, 16)
-        g.wait_ge(T.sem.qin, 16)
-        n = _send(g, T, topo, root, porter, T.qs[:], T.qs[:], T.sem.qin, on_only)
-        ids = [DstId(rid=topo.addr(d)[0], pnc=topo.addr(d)[1]) for d in direct]
-        g.remote_dma_fused([RemoteDMATransfer(dst_ids=ids, dma_engine_mask=off, remote_sem=T.sem.qin,
-                                              srcs=[T.qs[:]], dsts=[T.qs[:] for _ in direct])],
-                           local_sem=T.sem.sent)
-        n += _count(off)
+        g.sync.dma_start(T.qd[:], T.q[:]).then_inc(T.sem.qcp, 16)
+        g.wait_ge(T.sem.qcp, 16)
+        n = _send(g, T, topo, porter, T.qd[:], T.qd[:], T.sem.qin, q_on)
+        for col, _, via in groups:
+            if via == root:
+                n += _send(g, T, topo, col, T.qs[:], T.qd[:], T.sem.qin, topo.mask(root, col))
         g.sync.wait_ge(T.sem.sent, n)
         g.scalar.wait_ge(T.sem.sent, n)
-        _load_kv(g, T)
+        g.sync.dma_start(T.qs[:], T.q[:]).then_inc(T.sem.qin, 16)
+        g.sync.dma_start(T.kv[:, 0:W], T.k[:]).then_inc(T.sem.kld, 16)
+        g.scalar.dma_start(T.kv[:, W:SLOT], T.v[:]).then_inc(T.sem.vld, 16)
         g.wait_ge(T.sem.sent, n)
-        guest = 2 * _count(topo.mask(porter, root) & ~topo.mask(porter, collector))
-        _attend(g, T, 2, [(T.sem.qin, 16), (T.sem.kld, 16), (T.sem.vld, 16), (T.sem.guest, guest)])
+        passed = sum(_count(topo.mask(c, root)) for c in collectors)
+        _attend(g, T, [
+            ([(T.sem.qin, 16), (T.sem.kld, 16), (T.sem.vld, 16), (T.sem.guest, 2 * _count(porter_on))],
+             _slot_blocks(0) + _slot_blocks(1)),
+            ([(T.sem.passed, passed)],
+             [(2 * SLOT + i * 2 * P, 2 * SLOT + i * 2 * P + P) for i in range(len(collectors))]),
+        ])
         ve = g.vector
         prev = T.ops[:, 0:QP]
-        for i, s in enumerate(senders):
-            last = i == len(senders) - 1
+        for i, s in enumerate(collectors):
+            last = i == len(collectors) - 1
             ve.wait_ge(T.sem["land%d" % i], _count(topo.mask(s, root)))
             if i:
                 ve.wait_ge(T.sem.vadd, i)
             out = T.osb[:] if last else T.acc[:, i * QP:(i + 1) * QP]
             ve.tensor_tensor(out, prev, T.oland[:, i * QP:(i + 1) * QP], AluOpType.add).then_inc(T.sem.vadd, 1)
             prev = out
-        g.sync.wait_ge(T.sem.vadd, len(senders))
+        g.sync.wait_ge(T.sem.vadd, len(collectors))
         g.sync.dma_start(T.y[:], T.osb[:]).then_inc(T.sem.stored, 16)
         g.sync.wait_ge(T.sem.stored, 16)
 
     elif core == porter:
-        off = topo.mask(porter, collector)
-        on_only = topo.mask(porter, root) & ~off
-        _load_kv(g, T)
+        g.sync.dma_start(T.kv[:, 0:W], T.k[:]).then_inc(T.sem.kld, 16)
+        g.scalar.wait_ge(T.sem.kld, 16)
+        g.scalar.dma_start(T.kv[:, W:SLOT], T.v[:]).then_inc(T.sem.vld, 16)
         g.wait_ge(T.sem.kld, 16)
-        n = _send(g, T, topo, porter, root, T.kv[:, SLOT:SLOT + W], T.kv[:, 0:W], T.sem.guest, on_only)
-        g.wait_ge(T.sem.qin, _count(topo.mask(root, porter) & ~topo.mask(root, direct[0])))
-        n += _send(g, T, topo, porter, collector, T.qs[:], T.qs[:], T.sem.qin, off)
+        n = _send(g, T, topo, root, T.kv[:, SLOT:SLOT + W], T.kv[:, 0:W], T.sem.guest, porter_on)
+        g.wait_ge(T.sem.qin, _count(q_on))
+        for col in far:
+            n += _send(g, T, topo, col, T.qs[:], T.qd[:], T.sem.qin, topo.mask(porter, col))
         g.wait_ge(T.sem.vld, 16)
-        n += _send(g, T, topo, porter, root, T.kv[:, SLOT + W:2 * SLOT], T.kv[:, W:SLOT], T.sem.guest, on_only)
+        n += _send(g, T, topo, root, T.kv[:, SLOT + W:2 * SLOT], T.kv[:, W:SLOT], T.sem.guest, porter_on)
         g.wait_ge(T.sem.sent, n)
-
-    elif core in feeders:
-        _load_kv(g, T)
-        g.wait_ge(T.sem.kld, 16)
-        g.wait_ge(T.sem.vld, 16)
-        n = _send(g, T, topo, core, collector, T.kv[:, SLOT:2 * SLOT], T.kv[:, 0:SLOT], T.sem.guest,
-                  topo.mask(core, collector))
-        g.wait_ge(T.sem.sent, n)
-
-    elif core == collector:
-        _load_kv(g, T)
-        guest = sum(_count(topo.mask(f, collector)) for f in feeders)
-        _attend(g, T, 2, [(T.sem.kld, 16), (T.sem.vld, 16), (T.sem.guest, guest),
-                          (T.sem.qin, _count(topo.mask(porter, collector)))])
-        _return_result(g, T, topo, core, root, senders.index(core))
 
     else:
-        _load_kv(g, T)
-        _attend(g, T, 1, [(T.sem.kld, 16), (T.sem.vld, 16), (T.sem.qin, _count(topo.mask(root, core)))])
-        _return_result(g, T, topo, core, root, senders.index(core))
+        col, feeders, via = [gr for gr in groups if core == gr[0] or core in gr[1]][0]
+        g.sync.dma_start(T.kv[:, 0:W], T.k[:]).then_inc(T.sem.kld, 16)
+        g.scalar.dma_start(T.kv[:, W:SLOT], T.v[:]).then_inc(T.sem.vld, 16)
+        g.wait_ge(T.sem.kld, 16)
+        g.wait_ge(T.sem.vld, 16)
+        if core != col:
+            n = _send(g, T, topo, col, T.kv[:, SLOT:2 * SLOT], T.kv[:, 0:SLOT], T.sem.guest, topo.mask(core, col))
+            g.wait_ge(T.sem.sent, n)
+        else:
+            slot = collectors.index(col)
+            out = topo.mask(col, root)
+            half = _take(out, _count(out) // 2)
+            rid, pid, _ = topo.addr(root)
+            mine = _slot_blocks(0)
+            kc, vc = mine[-1]
+            base = 2 * SLOT + slot * 2 * P
+            g.remote_dma_fused([
+                RemoteDMATransfer(dst_ids=[DstId(rid=rid, pnc=pid)], dma_engine_mask=half, remote_sem=T.sem.passed,
+                                  src=T.kv[:, kc:kc + P], dst=T.kv[:, base:base + P]),
+                RemoteDMATransfer(dst_ids=[DstId(rid=rid, pnc=pid)], dma_engine_mask=out & ~half,
+                                  remote_sem=T.sem.passed, src=T.kv[:, vc:vc + P], dst=T.kv[:, base + P:base + 2 * P]),
+            ], local_sem=T.sem.sent)
+            n = _count(out)
+            guest = sum(_count(topo.mask(f, col)) for f in feeders)
+            _attend(g, T, [([(T.sem.kld, 16), (T.sem.vld, 16), (T.sem.guest, guest),
+                             (T.sem.qin, _count(topo.mask(via, col)))], mine[:-1] + _slot_blocks(1))])
+            g.vector.tensor_copy(T.osb[:], T.ops[:, 0:QP]).then_inc(T.sem.odone, 1)
+            g.wait_ge(T.sem.odone, 1)
+            n += _send(g, T, topo, root, T.oland[:, slot * QP:(slot + 1) * QP], T.osb[:],
+                       T.sem["land%d" % slot], out)
+            g.wait_ge(T.sem.sent, n)

from concourse.bass import DstId, RemoteDMATransfer
from concourse.mybir import AluOpType

P = 128
KB = 2
QP = 32
W = KB * P
SLOT = 2 * W
NLAND = 2
MAXB = 2 * KB + NLAND

SCRATCH = {
    "qd": ("dram", [P, QP], "bfloat16"),
    "qs": ("sbuf", [P, QP], "bfloat16"),
    "kv": ("sbuf", [P, 2 * SLOT + NLAND * 2 * P], "bfloat16"),
    "zero": ("sbuf", [P, MAXB * QP], "bfloat16"),
    "ssb": ("sbuf", [P, MAXB * QP], "bfloat16"),
    "osb": ("sbuf", [P, QP], "bfloat16"),
    "oland": ("sbuf", [P, NLAND * QP], "bfloat16"),
    "acc": ("sbuf", [P, NLAND * QP], "float32"),
    "sps0": ("psum", [P, 512], "float32"),
    "sps1": ("psum", [P, 512], "float32"),
    "ops": ("psum", [P, 512], "float32"),
}
SEMAPHORES = ["qcp", "qin", "kld", "vld", "guest", "passed", "sent", "zset", "mm1", "relu", "mm2", "odone", "vadd",
              "land0", "land1", "stored"]
Q_ENGINES = 4


def _count(mask):
    return bin(mask).count("1")


def _take(mask, n):
    bits = [i for i in range(mask.bit_length()) if (mask >> i) & 1][:n]
    return sum(1 << i for i in bits)


def _plan(T, topo):
    cores = list(T.cores)
    root = cores[T.root]
    porter = [c for c in cores if c != root and topo.chip(c) == topo.chip(root)][0]
    chips = []
    for c in cores:
        if topo.chip(c) != topo.chip(root) and topo.chip(c) not in chips:
            chips.append(topo.chip(c))
    groups = []
    for ch in chips:
        ranks = [c for c in cores if topo.chip(c) == ch]
        collector = [c for c in ranks if topo.may_write(c, root)][0]
        via = root if topo.may_write(root, collector) else porter
        groups.append((collector, [c for c in ranks if c != collector], via))
    groups.sort(key=lambda gr: gr[2] != root)
    return root, porter, groups


def _send(g, T, topo, dst, out_ap, in_ap, remote_sem, mask):
    rid, pid, _ = topo.addr(dst)
    g.remote_dma(out_ap, in_ap, remote_sem, T.sem.sent, pid, rid, mask)
    return _count(mask)


def _slot_blocks(s):
    return [(s * SLOT + b * P, s * SLOT + W + b * P) for b in range(KB)]


def _attend(g, T, batches):
    te, ve = g.tensor, g.vector
    total = sum(len(blocks) for _, blocks in batches)
    ve.memset(T.zero[:, 0:total * QP], 0.0).then_inc(T.sem.zset, 1)
    ve.wait_ge(T.sem.zset, 1)
    done = 0
    for i, (waits, blocks) in enumerate(batches):
        sps = T["sps%d" % i]
        nb = len(blocks)
        for sem, val in waits:
            te.wait_ge(sem, val)
        for j, (kc, _) in enumerate(blocks):
            te.matmul(sps[:, j * QP:(j + 1) * QP], T.kv[:, kc:kc + P], T.qs[:], start=True, stop=True).then_inc(T.sem.mm1, 1)
        ve.wait_ge(T.sem.mm1, done + nb)
        ve.tensor_tensor(T.ssb[:, done * QP:(done + nb) * QP], sps[:, 0:nb * QP], T.zero[:, 0:nb * QP],
                         AluOpType.max).then_inc(T.sem.relu, 1)
        te.wait_ge(T.sem.relu, i + 1)
        for j, (_, vc) in enumerate(blocks):
            n = done + j
            te.matmul(T.ops[:, 0:QP], T.kv[:, vc:vc + P], T.ssb[:, n * QP:(n + 1) * QP],
                      start=(n == 0), stop=(n == total - 1)).then_inc(T.sem.mm2, 1)
        done += nb
    ve.wait_ge(T.sem.mm2, total)


def rank_program(g, core, T, topo):
    if T.rank_of(core) is None:
        return
    root, porter, groups = _plan(T, topo)
    collectors = [gr[0] for gr in groups]
    far = [gr[0] for gr in groups if gr[2] == porter]
    q_on = _take(topo.mask(root, collectors[0]), Q_ENGINES)
    porter_on = topo.mask(porter, root) & ~topo.mask(porter, far[0])

    if core == root:
        g.sync.dma_start(T.qd[:], T.q[:]).then_inc(T.sem.qcp, 16)
        g.wait_ge(T.sem.qcp, 16)
        n = _send(g, T, topo, porter, T.qd[:], T.qd[:], T.sem.qin, q_on)
        for col, _, via in groups:
            if via == root:
                n += _send(g, T, topo, col, T.qs[:], T.qd[:], T.sem.qin, topo.mask(root, col))
        g.sync.wait_ge(T.sem.sent, n)
        g.scalar.wait_ge(T.sem.sent, n)
        g.sync.dma_start(T.qs[:], T.q[:]).then_inc(T.sem.qin, 16)
        g.sync.dma_start(T.kv[:, 0:W], T.k[:]).then_inc(T.sem.kld, 16)
        g.scalar.dma_start(T.kv[:, W:SLOT], T.v[:]).then_inc(T.sem.vld, 16)
        g.wait_ge(T.sem.sent, n)
        passed = sum(_count(topo.mask(c, root)) for c in collectors)
        _attend(g, T, [
            ([(T.sem.qin, 16), (T.sem.kld, 16), (T.sem.vld, 16), (T.sem.guest, 2 * _count(porter_on))],
             _slot_blocks(0) + _slot_blocks(1)),
            ([(T.sem.passed, passed)],
             [(2 * SLOT + i * 2 * P, 2 * SLOT + i * 2 * P + P) for i in range(len(collectors))]),
        ])
        ve = g.vector
        prev = T.ops[:, 0:QP]
        for i, s in enumerate(collectors):
            last = i == len(collectors) - 1
            ve.wait_ge(T.sem["land%d" % i], _count(topo.mask(s, root)))
            if i:
                ve.wait_ge(T.sem.vadd, i)
            out = T.osb[:] if last else T.acc[:, i * QP:(i + 1) * QP]
            ve.tensor_tensor(out, prev, T.oland[:, i * QP:(i + 1) * QP], AluOpType.add).then_inc(T.sem.vadd, 1)
            prev = out
        g.sync.wait_ge(T.sem.vadd, len(collectors))
        g.sync.dma_start(T.y[:], T.osb[:]).then_inc(T.sem.stored, 16)
        g.sync.wait_ge(T.sem.stored, 16)

    elif core == porter:
        g.sync.dma_start(T.kv[:, 0:W], T.k[:]).then_inc(T.sem.kld, 16)
        g.scalar.wait_ge(T.sem.kld, 16)
        g.scalar.dma_start(T.kv[:, W:SLOT], T.v[:]).then_inc(T.sem.vld, 16)
        g.wait_ge(T.sem.kld, 16)
        n = _send(g, T, topo, root, T.kv[:, SLOT:SLOT + W], T.kv[:, 0:W], T.sem.guest, porter_on)
        g.wait_ge(T.sem.qin, _count(q_on))
        for col in far:
            n += _send(g, T, topo, col, T.qs[:], T.qd[:], T.sem.qin, topo.mask(porter, col))
        g.wait_ge(T.sem.vld, 16)
        n += _send(g, T, topo, root, T.kv[:, SLOT + W:2 * SLOT], T.kv[:, W:SLOT], T.sem.guest, porter_on)
        g.wait_ge(T.sem.sent, n)

    else:
        col, feeders, via = [gr for gr in groups if core == gr[0] or core in gr[1]][0]
        g.sync.dma_start(T.kv[:, 0:W], T.k[:]).then_inc(T.sem.kld, 16)
        g.scalar.dma_start(T.kv[:, W:SLOT], T.v[:]).then_inc(T.sem.vld, 16)
        g.wait_ge(T.sem.kld, 16)
        g.wait_ge(T.sem.vld, 16)
        if core != col:
            n = _send(g, T, topo, col, T.kv[:, SLOT:2 * SLOT], T.kv[:, 0:SLOT], T.sem.guest, topo.mask(core, col))
            g.wait_ge(T.sem.sent, n)
        else:
            slot = collectors.index(col)
            out = topo.mask(col, root)
            half = _take(out, _count(out) // 2)
            rid, pid, _ = topo.addr(root)
            mine = _slot_blocks(0)
            kc, vc = mine[-1]
            base = 2 * SLOT + slot * 2 * P
            g.remote_dma_fused([
                RemoteDMATransfer(dst_ids=[DstId(rid=rid, pnc=pid)], dma_engine_mask=half, remote_sem=T.sem.passed,
                                  src=T.kv[:, kc:kc + P], dst=T.kv[:, base:base + P]),
                RemoteDMATransfer(dst_ids=[DstId(rid=rid, pnc=pid)], dma_engine_mask=out & ~half,
                                  remote_sem=T.sem.passed, src=T.kv[:, vc:vc + P], dst=T.kv[:, base + P:base + 2 * P]),
            ], local_sem=T.sem.sent)
            n = _count(out)
            guest = sum(_count(topo.mask(f, col)) for f in feeders)
            _attend(g, T, [([(T.sem.kld, 16), (T.sem.vld, 16), (T.sem.guest, guest),
                             (T.sem.qin, _count(topo.mask(via, col)))], mine[:-1] + _slot_blocks(1))])
            g.vector.tensor_copy(T.osb[:], T.ops[:, 0:QP]).then_inc(T.sem.odone, 1)
            g.wait_ge(T.sem.odone, 1)
            n += _send(g, T, topo, root, T.oland[:, slot * QP:(slot + 1) * QP], T.osb[:],
                       T.sem["land%d" % slot], out)
            g.wait_ge(T.sem.sent, n)
